import numpy as np
import ml_dtypes


def mxq(x, axis, fmt="e4m3"):
    dtype, down = {"e4m3": (ml_dtypes.float8_e4m3fn, 7), "e5m2": (ml_dtypes.float8_e5m2, 14)}[fmt]
    v = np.moveaxis(np.asarray(x, np.float32).astype(ml_dtypes.bfloat16).astype(np.float64), axis, -1)
    blocks = v.reshape(v.shape[:-1] + (-1, 32))
    amax = np.abs(blocks).max(-1, keepdims=True)
    byte = np.maximum(np.where(amax > 0, np.frexp(amax)[1] - 1 + 127, 0) - down, 1)
    scale = np.exp2(byte - 127.0)
    codes = (blocks / scale).astype(np.float32).astype(dtype).astype(np.float64)
    return np.moveaxis((codes * scale).reshape(v.shape), -1, axis)


WIDE = False


def mx_kscale(k, group=512):
    if not WIDE:
        return np.ones(k)
    levels = np.array([10, -10, 5, -5, 0])
    if group != 512:
        return np.exp2(np.random.permutation(np.resize(levels, k // group))).repeat(group)
    if k % 512:
        return np.exp2(np.random.permutation(np.resize(levels, k // 32))).repeat(32)
    a = np.empty((k // 512, 16))
    for p in range(k // 512):
        a[p, :8] = np.random.permutation(np.resize(levels, 8))
        for g in range(8):
            far = levels[np.abs(levels - a[p, g]) >= 10]
            a[p, g + 8] = far[np.random.randint(len(far))]
    return np.exp2(a.ravel()).repeat(32)


def f64(x):
    return np.asarray(x).astype(np.float64)


E2M1 = np.array([0.0, 0.5, 1.0, 1.5, 2.0, 3.0, 4.0, 6.0, -0.0, -0.5, -1.0, -1.5, -2.0, -3.0, -4.0, -6.0])


def pack_group(w):
    k, n = w.shape
    w = f64(np.asarray(w, np.float32).astype(ml_dtypes.bfloat16)).reshape(k // 32, 32, n)
    amax = np.abs(w).max(1)
    mant, ex = np.frexp(amax / 6.0)
    byte = np.clip(np.where(amax > 0, np.where(mant > 0.5, ex, ex - 1) + 127, 1), 1, 254)
    scaled = (w * np.exp2(127.0 - byte)[:, None, :]).reshape(k, n).astype(np.float32)
    c = np.ascontiguousarray(scaled.reshape(k // 4, 4, n).transpose(0, 2, 1)).astype(ml_dtypes.float4_e2m1fn).view(np.uint8) & 0xF
    return np.ascontiguousarray((c[..., 0::2] | (c[..., 1::2] << 4)).reshape(k // 4, 2 * n)), byte.astype(np.uint8)


def unpack_group(words, scales):
    p, n = words.shape[0], scales.shape[1]
    words = np.ascontiguousarray(words).reshape(p, n, 2)
    nib = np.empty((p, n, 4), np.uint8)
    nib[..., 0::2] = words & 0xF
    nib[..., 1::2] = words >> 4
    return E2M1[nib].transpose(0, 2, 1).reshape(4 * p, n) * np.repeat(np.exp2(scales.astype(np.float64) - 127.0), 32, axis=0)


G, D, M, O, N = 2, 256, 256, 256, 512


def setup_inputs():
    n = np.random.standard_normal
    s_d = mx_kscale(D, 0)
    s_o = mx_kscale(O, 0)
    w1_ = [pack_group(w) for w in n((G, D, M)) / np.sqrt(D) / s_d[:, None]]
    w2_ = [pack_group(w) for w in n((G, D, M)) / np.sqrt(D) / s_d[:, None]]
    wo_ = [pack_group(w) for w in n((G, O, M)) / np.sqrt(O) / s_o[:, None]]
    return {
        "x": (n((G, D, N)) * s_d[:, None]).astype(np.float32),
        "w1_words": np.stack([w[0] for w in w1_]),
        "w1_scales": np.stack([w[1] for w in w1_]),
        "w2_words": np.stack([w[0] for w in w2_]),
        "w2_scales": np.stack([w[1] for w in w2_]),
        "fl": (np.random.uniform(0.05, 0.3, (G, M, 1))).astype(np.float32),
        "wo_words": np.stack([w[0] for w in wo_]),
        "wo_scales": np.stack([w[1] for w in wo_]),
        "dy": (n((G, O, N)) * s_o[:, None]).astype(np.float32),
        "old": (0.3 * n((G, M, N))).astype(np.float32),
    }


def reference(x, w1_words, w1_scales, w2_words, w2_scales, fl, wo_words, wo_scales, dy, old):
    w1 = np.stack([unpack_group(w1_words[g], w1_scales[g]) for g in range(G)])
    xq = mxq(f64(x), 1, "e4m3")
    z1 = w1.transpose(0, 2, 1) @ xq
    w2 = np.stack([unpack_group(w2_words[g], w2_scales[g]) for g in range(G)])
    z2 = w2.transpose(0, 2, 1) @ xq
    e1 = np.exp(np.square(z1) * (-1.0))
    e2 = np.exp(np.square(z2) * (-1.0))
    wo = np.stack([unpack_group(wo_words[g], wo_scales[g]) for g in range(G)])
    dyq = mxq(f64(dy), 1, "e4m3")
    c0 = wo.transpose(0, 2, 1) @ dyq
    de1 = c0 * z2 / (e1 + e2 + f64(fl)) - c0 * z2 * e1 / np.square(e1 + e2 + f64(fl))
    dz1 = de1 * e1 * (-1.0) * z1 * 2.0
    y = dz1 + f64(old)
    return y

@@ -1,0 +1,207 @@
+from contextlib import ExitStack
+
+import concourse.mybir as mybir
+
+G, D, M, N = 2, 256, 256, 512
+FLOPS = 3 * 2 * G * D * M * N
+
+F32 = mybir.dt.float32
+BF16 = mybir.dt.bfloat16
+I32 = mybir.dt.int32
+U32 = mybir.dt.uint32
+U8 = mybir.dt.uint8
+FP8X4 = mybir.dt.float8_e4m3fn_x4
+FP4X4 = mybir.dt.float4_e2m1fn_x4
+ACT = mybir.ActivationFunctionType
+ALU = mybir.AluOpType
+
+P = 128
+PACK = 4
+ROWS = D // PACK
+HALF = N // 2
+W1, W2, WO = 0, 1, 2
+TILES = [(g, h) for h in range(M // P) for g in range(G)]
+X_VECTOR_COLS = 320
+SCALAR_SQUARES = 2
+
+
+def tile_rows_bgaussshare_kernel(tc, x, w1_words, w1_scales, w2_words, w2_scales, fl, wo_words, wo_scales, dy, old, out):
+    nc = tc.nc
+    with ExitStack() as ctx:
+        sb = ctx.enter_context(tc.tile_pool(name="sb", bufs=1))
+        ps = ctx.enter_context(tc.psum_pool(name="ps", bufs=1))
+        ctx.enter_context(tc.manual_schedule())
+
+        def f32_tiles(name):
+            return [sb.tile([P, N], F32, name="%s%d" % (name, i)) for i in range(len(TILES))]
+
+        x_raw = sb.tile([P, PACK, N], F32)
+        dy_raw = sb.tile([P, PACK, N], F32)
+        old_sb = sb.tile([P, len(TILES), N], F32)
+        words = [sb.tile([P, 2 * M], U8, name="words%d" % w, align_bytes=64) for w in (W1, W2, WO)]
+        scale_rows = sb.tile([4, 4, 3, M // 4], I32)
+        w_scale = sb.tile([P, 3, M], U8, align_bytes=64)
+        fl_rows = sb.tile([P, P], F32, align_bytes=64)
+        fl_cols = sb.tile([P, P], F32, align_bytes=64)
+
+        nc.vector.memset(fl_rows[:], 0.0)
+        nc.vector.memset(w_scale[:].rearrange("p w m -> p (w m)").bitcast(I32), 0)
+
+        nc.sync.dma_start(out=x_raw[:], in_=x.rearrange("g (p j) n -> (g p) j n", j=PACK))
+        for w, scales in ((W2, w2_scales), (W1, w1_scales), (WO, wo_scales)):
+            nc.scalar.dma_start(
+                out=scale_rows[:, :, w, :],
+                in_=scales.rearrange("g (a r) m -> r (g a) m", r=4).bitcast(I32),
+            )
+        nc.scalar.dma_start(
+            out=fl_rows[0:P:32, :].rearrange("q (t j) -> q t j", j=32),
+            in_=fl.rearrange("g (h q j) o -> q (g h) (j o)", q=4, j=32),
+        )
+
+        def load_words(w, dram):
+            nc.sync.dma_start(out=words[w][:].bitcast(I32), in_=dram.rearrange("g p b -> (g p) b").bitcast(I32))
+
+        load_words(W2, w2_words)
+        load_words(W1, w1_words)
+        nc.sync.dma_start(out=dy_raw[:], in_=dy.rearrange("g (p j) n -> (g p) j n", j=PACK))
+        load_words(WO, wo_words)
+        nc.sync.dma_start(out=old_sb[:], in_=old.rearrange("g (h p) n -> p (g h) n", p=P))
+
+        for q in range(4):
+            nc.vector.tensor_copy(
+                out=w_scale[32 * q : 32 * q + 4].rearrange("p w m -> p (w m)").bitcast(I32),
+                in_=scale_rows[:, q].rearrange("p w m -> p (w m)"),
+            )
+        nc.vector.transpose(out=fl_cols[:], in_=fl_rows[:])
+
+        def operand(name):
+            halves = [sb.tile([P, HALF, PACK], BF16, name="%s_bf%d" % (name, u), align_bytes=64) for u in range(2)]
+            codes = sb.tile([P, N], U32, name=name + "_codes", align_bytes=64)
+            plane = sb.tile([P, N], U8, name=name + "_plane", align_bytes=64)
+            return halves, codes, plane
+
+        def interleave(copy, halves, raw, c0, c1):
+            u = c0 // HALF
+            copy(
+                out=halves[u][:, c0 - u * HALF : c1 - u * HALF, :].rearrange("p (c i) j -> p c j i", i=4),
+                in_=raw[:, :, c0:c1].rearrange("p j (c i) -> p c j i", i=4),
+            )
+
+        def quantise(op, u):
+            halves, codes, plane = op
+            cols = slice(u * HALF, (u + 1) * HALF)
+            nc.vector.quantize_mx(
+                out=codes[:, cols].bitcast(FP8X4), scales=plane[:, cols], in_=halves[u][:].rearrange("p c j -> p (c j)")
+            )
+
+        xq = operand("x")
+        dyq = operand("dy")
+        interleave(nc.vector.tensor_copy, xq[0], x_raw, 0, HALF)
+        interleave(nc.scalar.copy, xq[0], x_raw, X_VECTOR_COLS, N)
+        interleave(nc.vector.tensor_copy, xq[0], x_raw, HALF, X_VECTOR_COLS)
+        quantise(xq, 0)
+        quantise(xq, 1)
+
+        bank_a = [ps.tile([P, N], F32, name="bank_a%d" % i) for i in range(len(TILES))]
+        bank_b = [ps.tile([P, N], F32, name="bank_b%d" % i) for i in range(len(TILES))]
+
+        def product(bank, w, op, i):
+            g, h = TILES[i]
+            rows = slice(ROWS * g, ROWS * (g + 1))
+            nc.tensor.matmul_mx(
+                out=bank[:],
+                lhsT=words[w][rows, 2 * P * h : 2 * P * (h + 1)].bitcast(FP4X4),
+                lhsT_scale=w_scale[rows, w, P * h : P * (h + 1)],
+                rhs=op[1][rows, :].bitcast(FP8X4),
+                rhs_scale=op[2][rows, :],
+                start=True,
+                stop=True,
+            )
+
+        for pair in ((0, 1), (2, 3)):
+            for i in pair:
+                product(bank_a[i], W2, xq, i)
+            for i in pair:
+                product(bank_b[i], W1, xq, i)
+
+        e2 = f32_tiles("e2")
+        z1 = f32_tiles("z1")
+        u = f32_tiles("u")
+        ln_a = f32_tiles("ln_a")
+        prod = f32_tiles("prod")
+        t2 = f32_tiles("t2")
+        y = f32_tiles("y")
+
+        def slot(i):
+            g, h = TILES[i]
+            return 2 * g + h
+
+        for pair in ((0, 1), (2, 3)):
+            for i in pair:
+                nc.scalar.activation(out=e2[i][:], in_=bank_a[i][:], func=ACT.Square)
+            for i in pair:
+                nc.scalar.activation(out=e2[i][:], in_=e2[i][:], func=ACT.Exp, scale=-1.0)
+
+        def copy_z1(i):
+            nc.vector.tensor_copy(out=z1[i][:], in_=bank_b[i][:])
+
+        def times_z2(i):
+            nc.vector.scalar_tensor_tensor(
+                out=prod[i][:], in0=bank_a[i][:], scalar=0.5, in1=z1[i][:], op0=ALU.mult, op1=ALU.mult
+            )
+
+        def times_c0(i):
+            nc.vector.tensor_tensor(out=prod[i][:], in0=bank_b[i][:], in1=prod[i][:], op=ALU.mult)
+
+        def square_z1(i):
+            nc.vector.tensor_tensor(out=u[i][:], in0=z1[i][:], in1=z1[i][:], op=ALU.mult)
+
+        def add_ln(i):
+            nc.vector.tensor_tensor(out=u[i][:], in0=u[i][:], in1=ln_a[i][:], op=ALU.add)
+
+        for pair in ((0, 1), (2, 3)):
+            for i in pair:
+                copy_z1(i)
+            if pair == (2, 3):
+                interleave(nc.vector.tensor_copy, dyq[0], dy_raw, 0, HALF)
+                interleave(nc.vector.tensor_copy, dyq[0], dy_raw, HALF, N)
+                quantise(dyq, 0)
+                quantise(dyq, 1)
+            for i in pair:
+                times_z2(i)
+        for i in range(len(TILES)):
+            product(bank_b[i], WO, dyq, i)
+
+        for i in range(SCALAR_SQUARES):
+            nc.scalar.activation(out=u[i][:], in_=z1[i][:], func=ACT.Square)
+        for i in range(len(TILES)):
+            k = 32 * slot(i)
+            nc.scalar.activation(out=ln_a[i][:], in_=e2[i][:], func=ACT.Ln, bias=fl_cols[:, k : k + 1])
+
+        for i in range(SCALAR_SQUARES, len(TILES)):
+            square_z1(i)
+        times_c0(0)
+        for i in range(len(TILES)):
+            add_ln(i)
+            if i == 0:
+                times_c0(1)
+        times_c0(2)
+        times_c0(3)
+
+        halves = (slice(0, HALF), slice(HALF, N))
+        for i in range(len(TILES)):
+            g, h = TILES[i]
+            for c in halves:
+                nc.scalar.activation(out=t2[i][:, c], in_=u[i][:, c], func=ACT.Tanh, scale=0.5)
+            for c in halves:
+                nc.scalar.activation(out=t2[i][:, c], in_=t2[i][:, c], func=ACT.Square)
+            for c in halves:
+                nc.vector.scalar_tensor_tensor(
+                    out=y[i][:, c], in0=t2[i][:, c], scalar=1.0, in1=prod[i][:, c], op0=ALU.subtract, op1=ALU.mult
+                )
+            for c in halves:
+                nc.vector.tensor_tensor(out=y[i][:, c], in0=y[i][:, c], in1=old_sb[:, slot(i), c], op=ALU.add)
+                if i == len(TILES) - 1:
+                    nc.sync.dma_start(out=out[g, P * h : P * (h + 1), c], in_=y[i][:, c])
+            if i < len(TILES) - 1:
+                nc.sync.dma_start(out=out[g, P * h : P * (h + 1), :], in_=y[i][:])

@@ -22,7 +22,7 @@ HALF = N // 2
 W1, W2, WO = 0, 1, 2
 TILES = [(g, h) for h in range(M // P) for g in range(G)]
 X_VECTOR_COLS = 320
-SCALAR_SQUARES = 2
+PAIRS = ((0, 1), (2, 3))
 
 
 def tile_rows_bgaussshare_kernel(tc, x, w1_words, w1_scales, w2_words, w2_scales, fl, wo_words, wo_scales, dy, old, out):
@@ -67,13 +67,6 @@ def tile_rows_bgaussshare_kernel(tc, x, w1_words, w1_scales, w2_words, w2_scales
         load_words(WO, wo_words)
         nc.sync.dma_start(out=old_sb[:], in_=old.rearrange("g (h p) n -> p (g h) n", p=P))
 
-        for q in range(4):
-            nc.vector.tensor_copy(
-                out=w_scale[32 * q : 32 * q + 4].rearrange("p w m -> p (w m)").bitcast(I32),
-                in_=scale_rows[:, q].rearrange("p w m -> p (w m)"),
-            )
-        nc.vector.transpose(out=fl_cols[:], in_=fl_rows[:])
-
         def operand(name):
             halves = [sb.tile([P, HALF, PACK], BF16, name="%s_bf%d" % (name, u), align_bytes=64) for u in range(2)]
             codes = sb.tile([P, N], U32, name=name + "_codes", align_bytes=64)
@@ -99,8 +92,14 @@ def tile_rows_bgaussshare_kernel(tc, x, w1_words, w1_scales, w2_words, w2_scales
         interleave(nc.vector.tensor_copy, xq[0], x_raw, 0, HALF)
         interleave(nc.scalar.copy, xq[0], x_raw, X_VECTOR_COLS, N)
         interleave(nc.vector.tensor_copy, xq[0], x_raw, HALF, X_VECTOR_COLS)
+        for q in range(4):
+            nc.vector.tensor_copy(
+                out=w_scale[32 * q : 32 * q + 4].rearrange("p w m -> p (w m)").bitcast(I32),
+                in_=scale_rows[:, q].rearrange("p w m -> p (w m)"),
+            )
         quantise(xq, 0)
         quantise(xq, 1)
+        nc.vector.transpose(out=fl_cols[:], in_=fl_rows[:])
 
         bank_a = [ps.tile([P, N], F32, name="bank_a%d" % i) for i in range(len(TILES))]
         bank_b = [ps.tile([P, N], F32, name="bank_b%d" % i) for i in range(len(TILES))]
@@ -118,11 +117,11 @@ def tile_rows_bgaussshare_kernel(tc, x, w1_words, w1_scales, w2_words, w2_scales
                 stop=True,
             )
 
-        for pair in ((0, 1), (2, 3)):
-            for i in pair:
-                product(bank_a[i], W2, xq, i)
-            for i in pair:
-                product(bank_b[i], W1, xq, i)
+        for a, b in PAIRS:
+            product(bank_a[a], W2, xq, a)
+            product(bank_b[b], W1, xq, b)
+            product(bank_a[b], W2, xq, b)
+            product(bank_b[a], W1, xq, a)
 
         e2 = f32_tiles("e2")
         z1 = f32_tiles("z1")
@@ -136,11 +135,12 @@ def tile_rows_bgaussshare_kernel(tc, x, w1_words, w1_scales, w2_words, w2_scales
             g, h = TILES[i]
             return 2 * g + h
 
-        for pair in ((0, 1), (2, 3)):
-            for i in pair:
-                nc.scalar.activation(out=e2[i][:], in_=bank_a[i][:], func=ACT.Square)
-            for i in pair:
-                nc.scalar.activation(out=e2[i][:], in_=e2[i][:], func=ACT.Exp, scale=-1.0)
+        halves = (slice(0, HALF), slice(HALF, N))
+        for i in range(len(TILES)):
+            for c in halves:
+                nc.scalar.activation(out=e2[i][:, c], in_=bank_a[i][:, c], func=ACT.Square)
+            for c in halves:
+                nc.scalar.activation(out=e2[i][:, c], in_=e2[i][:, c], func=ACT.Exp, scale=-1.0)
 
         def copy_z1(i):
             nc.vector.tensor_copy(out=z1[i][:], in_=bank_b[i][:])
@@ -153,33 +153,31 @@ def tile_rows_bgaussshare_kernel(tc, x, w1_words, w1_scales, w2_words, w2_scales
         def times_c0(i):
             nc.vector.tensor_tensor(out=prod[i][:], in0=bank_b[i][:], in1=prod[i][:], op=ALU.mult)
 
-        def square_z1(i):
-            nc.vector.tensor_tensor(out=u[i][:], in0=z1[i][:], in1=z1[i][:], op=ALU.mult)
+        def square_z1(i, c):
+            nc.vector.tensor_tensor(out=u[i][:, c], in0=z1[i][:, c], in1=z1[i][:, c], op=ALU.mult)
 
         def add_ln(i):
             nc.vector.tensor_tensor(out=u[i][:], in0=u[i][:], in1=ln_a[i][:], op=ALU.add)
 
-        for pair in ((0, 1), (2, 3)):
-            for i in pair:
-                copy_z1(i)
-            if pair == (2, 3):
-                interleave(nc.vector.tensor_copy, dyq[0], dy_raw, 0, HALF)
-                interleave(nc.vector.tensor_copy, dyq[0], dy_raw, HALF, N)
-                quantise(dyq, 0)
-                quantise(dyq, 1)
-            for i in pair:
-                times_z2(i)
+        for k, (a, b) in enumerate(PAIRS):
+            copy_z1(b)
+            interleave(nc.vector.tensor_copy, dyq[0], dy_raw, k * HALF, (k + 1) * HALF)
+            copy_z1(a)
+            quantise(dyq, k)
+            times_z2(b)
+            times_z2(a)
         for i in range(len(TILES)):
             product(bank_b[i], WO, dyq, i)
 
-        for i in range(SCALAR_SQUARES):
+        for i in range(2):
             nc.scalar.activation(out=u[i][:], in_=z1[i][:], func=ACT.Square)
+        nc.scalar.activation(out=u[3][:, halves[0]], in_=z1[3][:, halves[0]], func=ACT.Square)
         for i in range(len(TILES)):
             k = 32 * slot(i)
             nc.scalar.activation(out=ln_a[i][:], in_=e2[i][:], func=ACT.Ln, bias=fl_cols[:, k : k + 1])
 
-        for i in range(SCALAR_SQUARES, len(TILES)):
-            square_z1(i)
+        square_z1(2, slice(0, N))
+        square_z1(3, halves[1])
         times_c0(0)
         for i in range(len(TILES)):
             add_ln(i)
@@ -188,7 +186,6 @@ def tile_rows_bgaussshare_kernel(tc, x, w1_words, w1_scales, w2_words, w2_scales
         times_c0(2)
         times_c0(3)
 
-        halves = (slice(0, HALF), slice(HALF, N))
         for i in range(len(TILES)):
             g, h = TILES[i]
             for c in halves:

@@ -21,7 +21,6 @@ ROWS = D // PACK
 HALF = N // 2
 W1, W2, WO = 0, 1, 2
 TILES = [(g, h) for h in range(M // P) for g in range(G)]
-X_VECTOR_COLS = 320
 PAIRS = ((0, 1), (2, 3))
 
 
@@ -49,14 +48,10 @@ def tile_rows_bgaussshare_kernel(tc, x, w1_words, w1_scales, w2_words, w2_scales
 
         nc.sync.dma_start(out=x_raw[:], in_=x.rearrange("g (p j) n -> (g p) j n", j=PACK))
         for w, scales in ((W2, w2_scales), (W1, w1_scales), (WO, wo_scales)):
-            nc.scalar.dma_start(
+            nc.sync.dma_start(
                 out=scale_rows[:, :, w, :],
                 in_=scales.rearrange("g (a r) m -> r (g a) m", r=4).bitcast(I32),
             )
-        nc.scalar.dma_start(
-            out=fl_rows[0:P:32, :].rearrange("q (t j) -> q t j", j=32),
-            in_=fl.rearrange("g (h q j) o -> q (g h) (j o)", q=4, j=32),
-        )
 
         def load_words(w, dram):
             nc.sync.dma_start(out=words[w][:].bitcast(I32), in_=dram.rearrange("g p b -> (g p) b").bitcast(I32))
@@ -65,6 +60,10 @@ def tile_rows_bgaussshare_kernel(tc, x, w1_words, w1_scales, w2_words, w2_scales
         load_words(W1, w1_words)
         nc.sync.dma_start(out=dy_raw[:], in_=dy.rearrange("g (p j) n -> (g p) j n", j=PACK))
         load_words(WO, wo_words)
+        nc.sync.dma_start(
+            out=fl_rows[0:P:32, :].rearrange("q (t j) -> q t j", j=32),
+            in_=fl.rearrange("g (h q j) o -> q (g h) (j o)", q=4, j=32),
+        )
         nc.sync.dma_start(out=old_sb[:], in_=old.rearrange("g (h p) n -> p (g h) n", p=P))
 
         def operand(name):
@@ -90,8 +89,7 @@ def tile_rows_bgaussshare_kernel(tc, x, w1_words, w1_scales, w2_words, w2_scales
         xq = operand("x")
         dyq = operand("dy")
         interleave(nc.vector.tensor_copy, xq[0], x_raw, 0, HALF)
-        interleave(nc.scalar.copy, xq[0], x_raw, X_VECTOR_COLS, N)
-        interleave(nc.vector.tensor_copy, xq[0], x_raw, HALF, X_VECTOR_COLS)
+        interleave(nc.scalar.copy, xq[0], x_raw, HALF, N)
         for q in range(4):
             nc.vector.tensor_copy(
                 out=w_scale[32 * q : 32 * q + 4].rearrange("p w m -> p (w m)").bitcast(I32),
@@ -99,7 +97,11 @@ def tile_rows_bgaussshare_kernel(tc, x, w1_words, w1_scales, w2_words, w2_scales
             )
         quantise(xq, 0)
         quantise(xq, 1)
+        for k in range(2):
+            interleave(nc.vector.tensor_copy, dyq[0], dy_raw, k * HALF, (k + 1) * HALF)
         nc.vector.transpose(out=fl_cols[:], in_=fl_rows[:])
+        for k in range(2):
+            quantise(dyq, k)
 
         bank_a = [ps.tile([P, N], F32, name="bank_a%d" % i) for i in range(len(TILES))]
         bank_b = [ps.tile([P, N], F32, name="bank_b%d" % i) for i in range(len(TILES))]
@@ -119,9 +121,9 @@ def tile_rows_bgaussshare_kernel(tc, x, w1_words, w1_scales, w2_words, w2_scales
 
         for a, b in PAIRS:
             product(bank_a[a], W2, xq, a)
-            product(bank_b[b], W1, xq, b)
             product(bank_a[b], W2, xq, b)
             product(bank_b[a], W1, xq, a)
+            product(bank_b[b], W1, xq, b)
 
         e2 = f32_tiles("e2")
         z1 = f32_tiles("z1")
@@ -136,11 +138,11 @@ def tile_rows_bgaussshare_kernel(tc, x, w1_words, w1_scales, w2_words, w2_scales
             return 2 * g + h
 
         halves = (slice(0, HALF), slice(HALF, N))
-        for i in range(len(TILES)):
-            for c in halves:
-                nc.scalar.activation(out=e2[i][:, c], in_=bank_a[i][:, c], func=ACT.Square)
-            for c in halves:
-                nc.scalar.activation(out=e2[i][:, c], in_=e2[i][:, c], func=ACT.Exp, scale=-1.0)
+        for pair in PAIRS:
+            for i in pair:
+                nc.scalar.activation(out=e2[i][:], in_=bank_a[i][:], func=ACT.Square)
+            for i in pair:
+                nc.scalar.activation(out=e2[i][:], in_=e2[i][:], func=ACT.Exp, scale=-1.0)
 
         def copy_z1(i):
             nc.vector.tensor_copy(out=z1[i][:], in_=bank_b[i][:])
@@ -153,52 +155,38 @@ def tile_rows_bgaussshare_kernel(tc, x, w1_words, w1_scales, w2_words, w2_scales
         def times_c0(i):
             nc.vector.tensor_tensor(out=prod[i][:], in0=bank_b[i][:], in1=prod[i][:], op=ALU.mult)
 
-        def square_z1(i, c):
-            nc.vector.tensor_tensor(out=u[i][:, c], in0=z1[i][:, c], in1=z1[i][:, c], op=ALU.mult)
+        def square_z1(i):
+            nc.gpsimd.tensor_tensor(out=u[i][:], in0=z1[i][:], in1=z1[i][:], op=ALU.mult)
 
         def add_ln(i):
             nc.vector.tensor_tensor(out=u[i][:], in0=u[i][:], in1=ln_a[i][:], op=ALU.add)
 
-        for k, (a, b) in enumerate(PAIRS):
-            copy_z1(b)
-            interleave(nc.vector.tensor_copy, dyq[0], dy_raw, k * HALF, (k + 1) * HALF)
-            copy_z1(a)
-            quantise(dyq, k)
-            times_z2(b)
-            times_z2(a)
+        for pair in PAIRS:
+            for i in pair:
+                copy_z1(i)
+                square_z1(i)
+                product(bank_b[i], WO, dyq, i)
+            for i in pair:
+                times_z2(i)
         for i in range(len(TILES)):
-            product(bank_b[i], WO, dyq, i)
+            times_c0(i)
 
-        for i in range(2):
-            nc.scalar.activation(out=u[i][:], in_=z1[i][:], func=ACT.Square)
-        nc.scalar.activation(out=u[3][:, halves[0]], in_=z1[3][:, halves[0]], func=ACT.Square)
         for i in range(len(TILES)):
             k = 32 * slot(i)
             nc.scalar.activation(out=ln_a[i][:], in_=e2[i][:], func=ACT.Ln, bias=fl_cols[:, k : k + 1])
-
-        square_z1(2, slice(0, N))
-        square_z1(3, halves[1])
-        times_c0(0)
-        for i in range(len(TILES)):
             add_ln(i)
-            if i == 0:
-                times_c0(1)
-        times_c0(2)
-        times_c0(3)
 
-        for i in range(len(TILES)):
-            g, h = TILES[i]
-            for c in halves:
-                nc.scalar.activation(out=t2[i][:, c], in_=u[i][:, c], func=ACT.Tanh, scale=0.5)
-            for c in halves:
-                nc.scalar.activation(out=t2[i][:, c], in_=t2[i][:, c], func=ACT.Square)
-            for c in halves:
+        for pair in PAIRS:
+            for i in pair:
+                nc.scalar.activation(out=t2[i][:], in_=u[i][:], func=ACT.Tanh, scale=0.5)
+            for i in pair:
+                nc.scalar.activation(out=t2[i][:], in_=t2[i][:], func=ACT.Square)
+            for i in pair:
                 nc.vector.scalar_tensor_tensor(
-                    out=y[i][:, c], in0=t2[i][:, c], scalar=1.0, in1=prod[i][:, c], op0=ALU.subtract, op1=ALU.mult
+                    out=y[i][:], in0=t2[i][:], scalar=1.0, in1=prod[i][:], op0=ALU.subtract, op1=ALU.mult
                 )
-            for c in halves:
-                nc.vector.tensor_tensor(out=y[i][:, c], in0=y[i][:, c], in1=old_sb[:, slot(i), c], op=ALU.add)
-                if i == len(TILES) - 1:
+            for i in pair:
+                g, h = TILES[i]
+                for c in halves if i == len(TILES) - 1 else (slice(0, N),):
+                    nc.vector.tensor_tensor(out=y[i][:, c], in0=y[i][:, c], in1=old_sb[:, slot(i), c], op=ALU.add)
                     nc.sync.dma_start(out=out[g, P * h : P * (h + 1), c], in_=y[i][:, c])
-            if i < len(TILES) - 1:
-                nc.sync.dma_start(out=out[g, P * h : P * (h + 1), :], in_=y[i][:])

@@ -16,177 +16,183 @@ ACT = mybir.ActivationFunctionType
 ALU = mybir.AluOpType
 
 P = 128
+QUAD = 32
 PACK = 4
 ROWS = D // PACK
-HALF = N // 2
+SCALE_ROWS = 4
 W1, W2, WO = 0, 1, 2
 TILES = [(g, h) for h in range(M // P) for g in range(G)]
 PAIRS = ((0, 1), (2, 3))
+LAST = len(TILES) - 1
+HALF = N // 2
+HALVES = (slice(0, HALF), slice(HALF, N))
 
 
-def tile_rows_bgaussshare_kernel(tc, x, w1_words, w1_scales, w2_words, w2_scales, fl, wo_words, wo_scales, dy, old, out):
+def tile_rows_bgaussshare_kernel(
+    tc, x, w1_words, w1_scales, w2_words, w2_scales, fl, wo_words, wo_scales, dy, old, out
+):
     nc = tc.nc
     with ExitStack() as ctx:
         sb = ctx.enter_context(tc.tile_pool(name="sb", bufs=1))
         ps = ctx.enter_context(tc.psum_pool(name="ps", bufs=1))
         ctx.enter_context(tc.manual_schedule())
 
-        def f32_tiles(name):
-            return [sb.tile([P, N], F32, name="%s%d" % (name, i)) for i in range(len(TILES))]
-
         x_raw = sb.tile([P, PACK, N], F32)
         dy_raw = sb.tile([P, PACK, N], F32)
-        old_sb = sb.tile([P, len(TILES), N], F32)
+        old_sb = sb.tile([P, G, M // P, N], F32)
         words = [sb.tile([P, 2 * M], U8, name="words%d" % w, align_bytes=64) for w in (W1, W2, WO)]
-        scale_rows = sb.tile([4, 4, 3, M // 4], I32)
-        w_scale = sb.tile([P, 3, M], U8, align_bytes=64)
+        w_scale = sb.tile([P, P // QUAD, 3, M], U8, align_bytes=64)
         fl_rows = sb.tile([P, P], F32, align_bytes=64)
         fl_cols = sb.tile([P, P], F32, align_bytes=64)
 
-        nc.vector.memset(fl_rows[:], 0.0)
-        nc.vector.memset(w_scale[:].rearrange("p w m -> p (w m)").bitcast(I32), 0)
+        def scale_block(rows, q):
+            return w_scale[rows, q].rearrange("p w m -> p (w m)").bitcast(I32)
 
-        nc.sync.dma_start(out=x_raw[:], in_=x.rearrange("g (p j) n -> (g p) j n", j=PACK))
-        for w, scales in ((W2, w2_scales), (W1, w1_scales), (WO, wo_scales)):
-            nc.sync.dma_start(
-                out=scale_rows[:, :, w, :],
-                in_=scales.rearrange("g (a r) m -> r (g a) m", r=4).bitcast(I32),
-            )
+        nc.vector.memset(scale_block(slice(0, P), 0), 0)
+        nc.vector.memset(fl_rows[:], 0.0)
+
+        def load_operand(raw, dram):
+            nc.sync.dma_start(out=raw[:], in_=dram.rearrange("g (p j) n -> (g p) j n", j=PACK))
 
         def load_words(w, dram):
             nc.sync.dma_start(out=words[w][:].bitcast(I32), in_=dram.rearrange("g p b -> (g p) b").bitcast(I32))
 
+        load_operand(x_raw, x)
+        for w, scales in ((W2, w2_scales), (W1, w1_scales), (WO, wo_scales)):
+            nc.sync.dma_start(
+                out=w_scale[0:SCALE_ROWS, :, w, :].bitcast(I32),
+                in_=scales.rearrange("g (a r) m -> r (g a) m", r=SCALE_ROWS).bitcast(I32),
+            )
         load_words(W2, w2_words)
+        load_operand(dy_raw, dy)
         load_words(W1, w1_words)
-        nc.sync.dma_start(out=dy_raw[:], in_=dy.rearrange("g (p j) n -> (g p) j n", j=PACK))
         load_words(WO, wo_words)
         nc.sync.dma_start(
-            out=fl_rows[0:P:32, :].rearrange("q (t j) -> q t j", j=32),
-            in_=fl.rearrange("g (h q j) o -> q (g h) (j o)", q=4, j=32),
+            out=fl_rows[0:P:QUAD, :].rearrange("q (t j) -> q t j", j=QUAD),
+            in_=fl.rearrange("g (h q j) o -> q (g h) (j o)", q=P // QUAD, j=QUAD),
         )
-        nc.sync.dma_start(out=old_sb[:], in_=old.rearrange("g (h p) n -> p (g h) n", p=P))
+        nc.sync.dma_start(
+            out=old_sb[:].rearrange("p g h n -> p (g h) n"), in_=old.rearrange("g (h p) n -> p (g h) n", p=P)
+        )
 
-        def operand(name):
-            halves = [sb.tile([P, HALF, PACK], BF16, name="%s_bf%d" % (name, u), align_bytes=64) for u in range(2)]
+        def mx_tiles(name):
+            grouped = [sb.tile([P, HALF, PACK], BF16, name="%s_bf%d" % (name, k), align_bytes=64) for k in range(2)]
             codes = sb.tile([P, N], U32, name=name + "_codes", align_bytes=64)
             plane = sb.tile([P, N], U8, name=name + "_plane", align_bytes=64)
-            return halves, codes, plane
+            return grouped, codes, plane
 
-        def interleave(copy, halves, raw, c0, c1):
-            u = c0 // HALF
+        def interleave(copy, grouped, raw, k):
             copy(
-                out=halves[u][:, c0 - u * HALF : c1 - u * HALF, :].rearrange("p (c i) j -> p c j i", i=4),
-                in_=raw[:, :, c0:c1].rearrange("p j (c i) -> p c j i", i=4),
+                out=grouped[k][:].rearrange("p (c i) j -> p c j i", i=4),
+                in_=raw[:, :, HALVES[k]].rearrange("p j (c i) -> p c j i", i=4),
             )
 
-        def quantise(op, u):
-            halves, codes, plane = op
-            cols = slice(u * HALF, (u + 1) * HALF)
-            nc.vector.quantize_mx(
-                out=codes[:, cols].bitcast(FP8X4), scales=plane[:, cols], in_=halves[u][:].rearrange("p c j -> p (c j)")
-            )
+        def quantise(grouped, codes, plane):
+            for k, cols in enumerate(HALVES):
+                nc.vector.quantize_mx(
+                    out=codes[:, cols].bitcast(FP8X4),
+                    scales=plane[:, cols],
+                    in_=grouped[k][:].rearrange("p c j -> p (c j)"),
+                )
 
-        xq = operand("x")
-        dyq = operand("dy")
-        interleave(nc.vector.tensor_copy, xq[0], x_raw, 0, HALF)
-        interleave(nc.scalar.copy, xq[0], x_raw, HALF, N)
-        for q in range(4):
+        x_grouped, x_codes, x_plane = mx_tiles("x")
+        dy_grouped, dy_codes, dy_plane = mx_tiles("dy")
+        interleave(nc.vector.tensor_copy, x_grouped, x_raw, 0)
+        interleave(nc.scalar.copy, x_grouped, x_raw, 1)
+        for q in range(1, P // QUAD):
             nc.vector.tensor_copy(
-                out=w_scale[32 * q : 32 * q + 4].rearrange("p w m -> p (w m)").bitcast(I32),
-                in_=scale_rows[:, q].rearrange("p w m -> p (w m)"),
+                out=scale_block(slice(QUAD * q, QUAD * q + SCALE_ROWS), 0), in_=scale_block(slice(0, SCALE_ROWS), q)
             )
-        quantise(xq, 0)
-        quantise(xq, 1)
+        quantise(x_grouped, x_codes, x_plane)
         for k in range(2):
-            interleave(nc.vector.tensor_copy, dyq[0], dy_raw, k * HALF, (k + 1) * HALF)
+            interleave(nc.vector.tensor_copy, dy_grouped, dy_raw, k)
         nc.vector.transpose(out=fl_cols[:], in_=fl_rows[:])
-        for k in range(2):
-            quantise(dyq, k)
+        quantise(dy_grouped, dy_codes, dy_plane)
 
-        bank_a = [ps.tile([P, N], F32, name="bank_a%d" % i) for i in range(len(TILES))]
-        bank_b = [ps.tile([P, N], F32, name="bank_b%d" % i) for i in range(len(TILES))]
+        z2_bank = [ps.tile([P, N], F32, name="z2_bank%d" % i) for i in range(len(TILES))]
+        z1_c0_bank = [ps.tile([P, N], F32, name="z1_c0_bank%d" % i) for i in range(len(TILES))]
 
-        def product(bank, w, op, i):
+        def product(bank, w, codes, plane, i):
             g, h = TILES[i]
             rows = slice(ROWS * g, ROWS * (g + 1))
             nc.tensor.matmul_mx(
-                out=bank[:],
+                out=bank[i][:],
                 lhsT=words[w][rows, 2 * P * h : 2 * P * (h + 1)].bitcast(FP4X4),
-                lhsT_scale=w_scale[rows, w, P * h : P * (h + 1)],
-                rhs=op[1][rows, :].bitcast(FP8X4),
-                rhs_scale=op[2][rows, :],
+                lhsT_scale=w_scale[rows, 0, w, P * h : P * (h + 1)],
+                rhs=codes[rows, :].bitcast(FP8X4),
+                rhs_scale=plane[rows, :],
                 start=True,
                 stop=True,
             )
 
-        for a, b in PAIRS:
-            product(bank_a[a], W2, xq, a)
-            product(bank_a[b], W2, xq, b)
-            product(bank_b[a], W1, xq, a)
-            product(bank_b[b], W1, xq, b)
+        for i in range(len(TILES)):
+            product(z2_bank, W2, x_codes, x_plane, i)
+        for i in range(len(TILES)):
+            product(z1_c0_bank, W1, x_codes, x_plane, i)
 
-        e2 = f32_tiles("e2")
-        z1 = f32_tiles("z1")
-        u = f32_tiles("u")
-        ln_a = f32_tiles("ln_a")
-        prod = f32_tiles("prod")
-        t2 = f32_tiles("t2")
-        y = f32_tiles("y")
+        e2 = sb.tile([P, len(TILES), N], F32)
+        ln_a = sb.tile([P, len(TILES), N], F32)
+        u = sb.tile([P, len(TILES), N], F32)
+        z1 = sb.tile([P, len(TILES), N], F32)
+        prod = sb.tile([P, len(TILES), N], F32)
+        tanh2 = sb.tile([P, len(TILES), N], F32)
+        y = sb.tile([P, len(TILES), N], F32)
 
-        def slot(i):
-            g, h = TILES[i]
-            return 2 * g + h
+        def both(tile, pair):
+            return tile[:, pair[0] : pair[1] + 1, :].rearrange("p t n -> p (t n)")
 
-        halves = (slice(0, HALF), slice(HALF, N))
+        for i in range(len(TILES)):
+            nc.scalar.activation(out=e2[:, i], in_=z2_bank[i][:], func=ACT.Square)
         for pair in PAIRS:
-            for i in pair:
-                nc.scalar.activation(out=e2[i][:], in_=bank_a[i][:], func=ACT.Square)
-            for i in pair:
-                nc.scalar.activation(out=e2[i][:], in_=e2[i][:], func=ACT.Exp, scale=-1.0)
-
-        def copy_z1(i):
-            nc.vector.tensor_copy(out=z1[i][:], in_=bank_b[i][:])
-
-        def times_z2(i):
-            nc.vector.scalar_tensor_tensor(
-                out=prod[i][:], in0=bank_a[i][:], scalar=0.5, in1=z1[i][:], op0=ALU.mult, op1=ALU.mult
-            )
+            nc.scalar.activation(out=both(e2, pair), in_=both(e2, pair), func=ACT.Exp, scale=-1.0)
+        for i, (g, h) in enumerate(TILES):
+            col = QUAD * (g * (M // P) + h)
+            nc.scalar.activation(out=ln_a[:, i], in_=e2[:, i], func=ACT.Ln, bias=fl_cols[:, col : col + 1])
 
         def times_c0(i):
-            nc.vector.tensor_tensor(out=prod[i][:], in0=bank_b[i][:], in1=prod[i][:], op=ALU.mult)
+            nc.vector.tensor_tensor(out=prod[:, i], in0=z1_c0_bank[i][:], in1=prod[:, i], op=ALU.mult)
 
-        def square_z1(i):
-            nc.gpsimd.tensor_tensor(out=u[i][:], in0=z1[i][:], in1=z1[i][:], op=ALU.mult)
-
-        def add_ln(i):
-            nc.vector.tensor_tensor(out=u[i][:], in0=u[i][:], in1=ln_a[i][:], op=ALU.add)
+        def add_ln(pair):
+            nc.vector.tensor_tensor(out=both(u, pair), in0=both(u, pair), in1=both(ln_a, pair), op=ALU.add)
 
         for pair in PAIRS:
             for i in pair:
-                copy_z1(i)
-                square_z1(i)
-                product(bank_b[i], WO, dyq, i)
-            for i in pair:
-                times_z2(i)
-        for i in range(len(TILES)):
-            times_c0(i)
-
-        for i in range(len(TILES)):
-            k = 32 * slot(i)
-            nc.scalar.activation(out=ln_a[i][:], in_=e2[i][:], func=ACT.Ln, bias=fl_cols[:, k : k + 1])
-            add_ln(i)
-
-        for pair in PAIRS:
-            for i in pair:
-                nc.scalar.activation(out=t2[i][:], in_=u[i][:], func=ACT.Tanh, scale=0.5)
-            for i in pair:
-                nc.scalar.activation(out=t2[i][:], in_=t2[i][:], func=ACT.Square)
+                nc.vector.tensor_copy(out=z1[:, i], in_=z1_c0_bank[i][:])
+                nc.gpsimd.tensor_tensor(out=u[:, i], in0=z1[:, i], in1=z1[:, i], op=ALU.mult)
+                product(z1_c0_bank, WO, dy_codes, dy_plane, i)
             for i in pair:
                 nc.vector.scalar_tensor_tensor(
-                    out=y[i][:], in0=t2[i][:], scalar=1.0, in1=prod[i][:], op0=ALU.subtract, op1=ALU.mult
+                    out=prod[:, i], in0=z2_bank[i][:], scalar=0.5, in1=z1[:, i], op0=ALU.mult, op1=ALU.mult
                 )
+        for i in range(LAST):
+            times_c0(i)
+        add_ln(PAIRS[0])
+        times_c0(LAST)
+        add_ln(PAIRS[1])
+
+        def weigh(i, cols):
+            nc.vector.scalar_tensor_tensor(
+                out=y[:, i, cols], in0=tanh2[:, i, cols], scalar=1.0, in1=prod[:, i, cols], op0=ALU.subtract, op1=ALU.mult
+            )
+
+        def finish(i, cols):
+            g, h = TILES[i]
+            nc.vector.tensor_tensor(out=y[:, i, cols], in0=y[:, i, cols], in1=old_sb[:, g, h, cols], op=ALU.add)
+            nc.sync.dma_start(out=out[g, P * h : P * (h + 1), cols], in_=y[:, i, cols])
+
+        for pair in PAIRS:
             for i in pair:
-                g, h = TILES[i]
-                for c in halves if i == len(TILES) - 1 else (slice(0, N),):
-                    nc.vector.tensor_tensor(out=y[i][:, c], in0=y[i][:, c], in1=old_sb[:, slot(i), c], op=ALU.add)
-                    nc.sync.dma_start(out=out[g, P * h : P * (h + 1), c], in_=y[i][:, c])
+                nc.scalar.activation(out=tanh2[:, i], in_=u[:, i], func=ACT.Tanh, scale=0.5)
+            for i in pair:
+                nc.scalar.activation(out=tanh2[:, i], in_=tanh2[:, i], func=ACT.Square)
+        whole = slice(0, N)
+        for i in PAIRS[0]:
+            weigh(i, whole)
+        for i in PAIRS[0]:
+            finish(i, whole)
+        weigh(LAST - 1, whole)
+        weigh(LAST, HALVES[0])
+        finish(LAST - 1, whole)
+        weigh(LAST, HALVES[1])
+        for cols in HALVES:
+            finish(LAST, cols)

@@ -26,6 +26,7 @@ PAIRS = ((0, 1), (2, 3))
 LAST = len(TILES) - 1
 HALF = N // 2
 HALVES = (slice(0, HALF), slice(HALF, N))
+X_SPLIT = 320
 
 
 def tile_rows_bgaussshare_kernel(
@@ -64,13 +65,13 @@ def tile_rows_bgaussshare_kernel(
                 in_=scales.rearrange("g (a r) m -> r (g a) m", r=SCALE_ROWS).bitcast(I32),
             )
         load_words(W2, w2_words)
-        load_operand(dy_raw, dy)
-        load_words(W1, w1_words)
-        load_words(WO, wo_words)
         nc.sync.dma_start(
             out=fl_rows[0:P:QUAD, :].rearrange("q (t j) -> q t j", j=QUAD),
             in_=fl.rearrange("g (h q j) o -> q (g h) (j o)", q=P // QUAD, j=QUAD),
         )
+        load_operand(dy_raw, dy)
+        load_words(W1, w1_words)
+        load_words(WO, wo_words)
         nc.sync.dma_start(
             out=old_sb[:].rearrange("p g h n -> p (g h) n"), in_=old.rearrange("g (h p) n -> p (g h) n", p=P)
         )
@@ -81,10 +82,11 @@ def tile_rows_bgaussshare_kernel(
             plane = sb.tile([P, N], U8, name=name + "_plane", align_bytes=64)
             return grouped, codes, plane
 
-        def interleave(copy, grouped, raw, k):
+        def interleave(copy, grouped, raw, start, stop):
+            k = start // HALF
             copy(
-                out=grouped[k][:].rearrange("p (c i) j -> p c j i", i=4),
-                in_=raw[:, :, HALVES[k]].rearrange("p j (c i) -> p c j i", i=4),
+                out=grouped[k][:, start - k * HALF : stop - k * HALF].rearrange("p (c i) j -> p c j i", i=4),
+                in_=raw[:, :, start:stop].rearrange("p j (c i) -> p c j i", i=4),
             )
 
         def quantise(grouped, codes, plane):
@@ -95,18 +97,23 @@ def tile_rows_bgaussshare_kernel(
                     in_=grouped[k][:].rearrange("p c j -> p (c j)"),
                 )
 
-        x_grouped, x_codes, x_plane = mx_tiles("x")
-        dy_grouped, dy_codes, dy_plane = mx_tiles("dy")
-        interleave(nc.vector.tensor_copy, x_grouped, x_raw, 0)
-        interleave(nc.scalar.copy, x_grouped, x_raw, 1)
-        for q in range(1, P // QUAD):
+        def place_scales(q):
             nc.vector.tensor_copy(
                 out=scale_block(slice(QUAD * q, QUAD * q + SCALE_ROWS), 0), in_=scale_block(slice(0, SCALE_ROWS), q)
             )
+
+        x_grouped, x_codes, x_plane = mx_tiles("x")
+        dy_grouped, dy_codes, dy_plane = mx_tiles("dy")
+        interleave(nc.vector.tensor_copy, x_grouped, x_raw, 0, HALF)
+        interleave(nc.vector.tensor_copy, x_grouped, x_raw, HALF, X_SPLIT)
+        interleave(nc.scalar.copy, x_grouped, x_raw, X_SPLIT, N)
+        place_scales(1)
         quantise(x_grouped, x_codes, x_plane)
-        for k in range(2):
-            interleave(nc.vector.tensor_copy, dy_grouped, dy_raw, k)
+        place_scales(2)
+        place_scales(3)
         nc.vector.transpose(out=fl_cols[:], in_=fl_rows[:])
+        for cols in HALVES:
+            interleave(nc.vector.tensor_copy, dy_grouped, dy_raw, cols.start, cols.stop)
         quantise(dy_grouped, dy_codes, dy_plane)
 
         z2_bank = [ps.tile([P, N], F32, name="z2_bank%d" % i) for i in range(len(TILES))]
@@ -180,14 +187,20 @@ def tile_rows_bgaussshare_kernel(
             nc.vector.tensor_tensor(out=y[:, i, cols], in0=y[:, i, cols], in1=old_sb[:, g, h, cols], op=ALU.add)
             nc.sync.dma_start(out=out[g, P * h : P * (h + 1), cols], in_=y[:, i, cols])
 
+        whole = slice(0, N)
         for pair in PAIRS:
             for i in pair:
                 nc.scalar.activation(out=tanh2[:, i], in_=u[:, i], func=ACT.Tanh, scale=0.5)
             for i in pair:
-                nc.scalar.activation(out=tanh2[:, i], in_=tanh2[:, i], func=ACT.Square)
-        whole = slice(0, N)
-        for i in PAIRS[0]:
-            weigh(i, whole)
+                cols = HALVES[1] if i == 0 else whole
+                nc.scalar.activation(out=tanh2[:, i, cols], in_=tanh2[:, i, cols], func=ACT.Square)
+        for cols in HALVES:
+            weigh(0, cols)
+        first = HALVES[0]
+        nc.vector.scalar_tensor_tensor(
+            out=y[:, 0, first], in0=tanh2[:, 0, first], scalar=1.0, in1=y[:, 0, first], op0=ALU.add, op1=ALU.mult
+        )
+        weigh(1, whole)
         for i in PAIRS[0]:
             finish(i, whole)
         weigh(LAST - 1, whole)

from contextlib import ExitStack

import concourse.mybir as mybir

G, D, M, N = 2, 256, 256, 512
FLOPS = 3 * 2 * G * D * M * N

F32 = mybir.dt.float32
BF16 = mybir.dt.bfloat16
I32 = mybir.dt.int32
U32 = mybir.dt.uint32
U8 = mybir.dt.uint8
FP8X4 = mybir.dt.float8_e4m3fn_x4
FP4X4 = mybir.dt.float4_e2m1fn_x4
ACT = mybir.ActivationFunctionType
ALU = mybir.AluOpType

P = 128
QUAD = 32
PACK = 4
ROWS = D // PACK
SCALE_ROWS = 4
W1, W2, WO = 0, 1, 2
TILES = [(g, h) for h in range(M // P) for g in range(G)]
PAIRS = ((0, 1), (2, 3))
LAST = len(TILES) - 1
HALF = N // 2
HALVES = (slice(0, HALF), slice(HALF, N))
X_SPLIT = 320


def tile_rows_bgaussshare_kernel(
    tc, x, w1_words, w1_scales, w2_words, w2_scales, fl, wo_words, wo_scales, dy, old, out
):
    nc = tc.nc
    with ExitStack() as ctx:
        sb = ctx.enter_context(tc.tile_pool(name="sb", bufs=1))
        ps = ctx.enter_context(tc.psum_pool(name="ps", bufs=1))
        ctx.enter_context(tc.manual_schedule())

        x_raw = sb.tile([P, PACK, N], F32)
        dy_raw = sb.tile([P, PACK, N], F32)
        old_sb = sb.tile([P, G, M // P, N], F32)
        words = [sb.tile([P, 2 * M], U8, name="words%d" % w, align_bytes=64) for w in (W1, W2, WO)]
        w_scale = sb.tile([P, P // QUAD, 3, M], U8, align_bytes=64)
        fl_rows = sb.tile([P, P], F32, align_bytes=64)
        fl_cols = sb.tile([P, P], F32, align_bytes=64)

        def scale_block(rows, q):
            return w_scale[rows, q].rearrange("p w m -> p (w m)").bitcast(I32)

        nc.vector.memset(scale_block(slice(0, P), 0), 0)
        nc.vector.memset(fl_rows[:], 0.0)

        def load_operand(raw, dram):
            nc.sync.dma_start(out=raw[:], in_=dram.rearrange("g (p j) n -> (g p) j n", j=PACK))

        def load_words(w, dram):
            nc.sync.dma_start(out=words[w][:].bitcast(I32), in_=dram.rearrange("g p b -> (g p) b").bitcast(I32))

        load_operand(x_raw, x)
        for w, scales in ((W2, w2_scales), (W1, w1_scales), (WO, wo_scales)):
            nc.sync.dma_start(
                out=w_scale[0:SCALE_ROWS, :, w, :].bitcast(I32),
                in_=scales.rearrange("g (a r) m -> r (g a) m", r=SCALE_ROWS).bitcast(I32),
            )
        load_words(W2, w2_words)
        nc.sync.dma_start(
            out=fl_rows[0:P:QUAD, :].rearrange("q (t j) -> q t j", j=QUAD),
            in_=fl.rearrange("g (h q j) o -> q (g h) (j o)", q=P // QUAD, j=QUAD),
        )
        load_operand(dy_raw, dy)
        load_words(W1, w1_words)
        load_words(WO, wo_words)
        nc.sync.dma_start(
            out=old_sb[:].rearrange("p g h n -> p (g h) n"), in_=old.rearrange("g (h p) n -> p (g h) n", p=P)
        )

        def mx_tiles(name):
            grouped = [sb.tile([P, HALF, PACK], BF16, name="%s_bf%d" % (name, k), align_bytes=64) for k in range(2)]
            codes = sb.tile([P, N], U32, name=name + "_codes", align_bytes=64)
            plane = sb.tile([P, N], U8, name=name + "_plane", align_bytes=64)
            return grouped, codes, plane

        def interleave(copy, grouped, raw, start, stop):
            k = start // HALF
            copy(
                out=grouped[k][:, start - k * HALF : stop - k * HALF].rearrange("p (c i) j -> p c j i", i=4),
                in_=raw[:, :, start:stop].rearrange("p j (c i) -> p c j i", i=4),
            )

        def quantise(grouped, codes, plane):
            for k, cols in enumerate(HALVES):
                nc.vector.quantize_mx(
                    out=codes[:, cols].bitcast(FP8X4),
                    scales=plane[:, cols],
                    in_=grouped[k][:].rearrange("p c j -> p (c j)"),
                )

        def place_scales(q):
            nc.vector.tensor_copy(
                out=scale_block(slice(QUAD * q, QUAD * q + SCALE_ROWS), 0), in_=scale_block(slice(0, SCALE_ROWS), q)
            )

        x_grouped, x_codes, x_plane = mx_tiles("x")
        dy_grouped, dy_codes, dy_plane = mx_tiles("dy")
        interleave(nc.vector.tensor_copy, x_grouped, x_raw, 0, HALF)
        interleave(nc.vector.tensor_copy, x_grouped, x_raw, HALF, X_SPLIT)
        interleave(nc.scalar.copy, x_grouped, x_raw, X_SPLIT, N)
        place_scales(1)
        quantise(x_grouped, x_codes, x_plane)
        place_scales(2)
        place_scales(3)
        nc.vector.transpose(out=fl_cols[:], in_=fl_rows[:])
        for cols in HALVES:
            interleave(nc.vector.tensor_copy, dy_grouped, dy_raw, cols.start, cols.stop)
        quantise(dy_grouped, dy_codes, dy_plane)

        z2_bank = [ps.tile([P, N], F32, name="z2_bank%d" % i) for i in range(len(TILES))]
        z1_c0_bank = [ps.tile([P, N], F32, name="z1_c0_bank%d" % i) for i in range(len(TILES))]

        def product(bank, w, codes, plane, i):
            g, h = TILES[i]
            rows = slice(ROWS * g, ROWS * (g + 1))
            nc.tensor.matmul_mx(
                out=bank[i][:],
                lhsT=words[w][rows, 2 * P * h : 2 * P * (h + 1)].bitcast(FP4X4),
                lhsT_scale=w_scale[rows, 0, w, P * h : P * (h + 1)],
                rhs=codes[rows, :].bitcast(FP8X4),
                rhs_scale=plane[rows, :],
                start=True,
                stop=True,
            )

        for i in range(len(TILES)):
            product(z2_bank, W2, x_codes, x_plane, i)
        for i in range(len(TILES)):
            product(z1_c0_bank, W1, x_codes, x_plane, i)

        e2 = sb.tile([P, len(TILES), N], F32)
        ln_a = sb.tile([P, len(TILES), N], F32)
        u = sb.tile([P, len(TILES), N], F32)
        z1 = sb.tile([P, len(TILES), N], F32)
        prod = sb.tile([P, len(TILES), N], F32)
        tanh2 = sb.tile([P, len(TILES), N], F32)
        y = sb.tile([P, len(TILES), N], F32)

        def both(tile, pair):
            return tile[:, pair[0] : pair[1] + 1, :].rearrange("p t n -> p (t n)")

        for i in range(len(TILES)):
            nc.scalar.activation(out=e2[:, i], in_=z2_bank[i][:], func=ACT.Square)
        for pair in PAIRS:
            nc.scalar.activation(out=both(e2, pair), in_=both(e2, pair), func=ACT.Exp, scale=-1.0)
        for i, (g, h) in enumerate(TILES):
            col = QUAD * (g * (M // P) + h)
            nc.scalar.activation(out=ln_a[:, i], in_=e2[:, i], func=ACT.Ln, bias=fl_cols[:, col : col + 1])

        def times_c0(i):
            nc.vector.tensor_tensor(out=prod[:, i], in0=z1_c0_bank[i][:], in1=prod[:, i], op=ALU.mult)

        def add_ln(pair):
            nc.vector.tensor_tensor(out=both(u, pair), in0=both(u, pair), in1=both(ln_a, pair), op=ALU.add)

        for pair in PAIRS:
            for i in pair:
                nc.vector.tensor_copy(out=z1[:, i], in_=z1_c0_bank[i][:])
                nc.gpsimd.tensor_tensor(out=u[:, i], in0=z1[:, i], in1=z1[:, i], op=ALU.mult)
                product(z1_c0_bank, WO, dy_codes, dy_plane, i)
            for i in pair:
                nc.vector.scalar_tensor_tensor(
                    out=prod[:, i], in0=z2_bank[i][:], scalar=0.5, in1=z1[:, i], op0=ALU.mult, op1=ALU.mult
                )
        for i in range(LAST):
            times_c0(i)
        add_ln(PAIRS[0])
        times_c0(LAST)
        add_ln(PAIRS[1])

        def weigh(i, cols):
            nc.vector.scalar_tensor_tensor(
                out=y[:, i, cols], in0=tanh2[:, i, cols], scalar=1.0, in1=prod[:, i, cols], op0=ALU.subtract, op1=ALU.mult
            )

        def finish(i, cols):
            g, h = TILES[i]
            nc.vector.tensor_tensor(out=y[:, i, cols], in0=y[:, i, cols], in1=old_sb[:, g, h, cols], op=ALU.add)
            nc.sync.dma_start(out=out[g, P * h : P * (h + 1), cols], in_=y[:, i, cols])

        whole = slice(0, N)
        for pair in PAIRS:
            for i in pair:
                nc.scalar.activation(out=tanh2[:, i], in_=u[:, i], func=ACT.Tanh, scale=0.5)
            for i in pair:
                cols = HALVES[1] if i == 0 else whole
                nc.scalar.activation(out=tanh2[:, i, cols], in_=tanh2[:, i, cols], func=ACT.Square)
        for cols in HALVES:
            weigh(0, cols)
        first = HALVES[0]
        nc.vector.scalar_tensor_tensor(
            out=y[:, 0, first], in0=tanh2[:, 0, first], scalar=1.0, in1=y[:, 0, first], op0=ALU.add, op1=ALU.mult
        )
        weigh(1, whole)
        for i in PAIRS[0]:
            finish(i, whole)
        weigh(LAST - 1, whole)
        weigh(LAST, HALVES[0])
        finish(LAST - 1, whole)
        weigh(LAST, HALVES[1])
        for cols in HALVES:
            finish(LAST, cols)
